import numpy as np
CORES = [0,1,2,3,4,5,6,7,128,129,130,131,132,133,134,135,256,257,258,259,260,261,262,263,384,385,386,387,388,389,390,391]
N = 32
GROUPS = [[0,8,16,24],[1,9,17,25],[2,10,18,26],[3,11,19,27],[4,12,20,28],[5,13,21,29],[6,14,22,30],[7,15,23,31]]
def setup_inputs(rng):
    return {"x": rng.standard_normal((N, 128, 1024), dtype=np.float32)}
def reference(x):
    y = np.empty((N, 128, 1024), x.dtype)
    for g in GROUPS:
        s = x[g].max(axis=0)
        for r in g:
            y[r] = s
    return {"y": y}

from concourse.bass import DstId, RemoteDMATransfer

NCH = 16
HALF = NCH // 2
W = 64
SCRATCH = {
    "buf": ("dram", [NCH, 128, W], "float32"),
    "opa": ("dram", [128, W], "float32"),
    "opb": ("dram", [128, W], "float32"),
    "pc": ("dram", [128, W], "float32"),
}
SEMAPHORES = ["ld0", "ld1", "s_op", "s_pc", "s_res0", "s_res1", "s_loc", "st"]
OFF_CHIP = 0x00FF
MAX = 2


def rank_program(g, core, T, topo):
    if topo.chip(core) % 2:
        return
    sem = T.sem
    h = topo.host(core)
    rank = T.rank_of(core)
    groups = [{topo.host(T.cores[r]): T.cores[r] for r in grp} for grp in T.tables["GROUPS"]]

    def did(dst):
        rid, pid = topo.addr(dst, core)
        return DstId(rid=rid, pnc=pid)

    def side(host):
        return host if topo.rack(host) == 0 else 3 - host

    def reducer(at, host, k):
        return host * 128 + 2 * (k % HALF) * 8 + ((at[host] % 8) ^ 1)

    left = 0

    if rank is not None:
        at = [a for a in groups if a[h] == core][0]
        g.sync.dma_start(T.buf[0:HALF], T.x[0:64, :]).then_inc(sem.ld0, 16)
        g.scalar.dma_start(T.buf[HALF:NCH], T.x[64:128, :]).then_inc(sem.ld1, 16)
        for half, loaded in ((0, sem.ld0), (1, sem.ld1)):
            a = h if side(h) == half else h ^ 1
            g.wait_ge(loaded, 16)
            g.remote_dma_fused([
                RemoteDMATransfer(dst_ids=[did(reducer(at, a, half * HALF + e))], dma_engine_mask=1 << e,
                                  remote_sem=sem.s_op, src=T.buf[half * HALF + e],
                                  dst=(T.opa[:] if a == h else T.opb[:]))
                for e in range(HALF)], local_sem=sem.s_loc)
            left += HALF

    k = side(h) * HALF + topo.chip(core) // 2
    at = [a for a in groups if (a[h] % 8) ^ 1 == core % 8][0]
    g.wait_ge(sem.s_op, 2)
    g.remote_dma_fused([
        RemoteDMATransfer(dst_ids=[did(reducer(at, 3 - h, k))], dma_engine_mask=OFF_CHIP, remote_sem=sem.s_pc,
                          srcs=[T.opa[:], T.opb[:]], dsts=[T.pc[:]], alu_op=MAX)], local_sem=sem.s_loc)
    g.wait_ge(sem.s_pc, 8)
    g.remote_dma_fused([
        RemoteDMATransfer(dst_ids=[did(at[h]), did(at[h ^ 1])], dma_engine_mask=OFF_CHIP,
                          remote_sem=(sem.s_res0 if k < HALF else sem.s_res1),
                          srcs=[T.opa[:], T.opb[:], T.pc[:]], dsts=[T.buf[k], T.buf[k]], alu_op=MAX)],
        local_sem=sem.s_loc)
    left += 16

    if rank is not None:
        g.sync.wait_ge(sem.s_res0, 8 * HALF)
        g.sync.dma_start(T.y[0:64, :], T.buf[0:HALF]).then_inc(sem.st, 16)
        g.scalar.wait_ge(sem.s_res1, 8 * HALF)
        g.scalar.dma_start(T.y[64:128, :], T.buf[HALF:NCH]).then_inc(sem.st, 16)
        g.wait_ge(sem.st, 32)
    g.wait_ge(sem.s_loc, left)
